import numpy as np
import ml_dtypes


def mxq(x, axis, fmt="e4m3"):
    dtype, down = {"e4m3": (ml_dtypes.float8_e4m3fn, 7), "e5m2": (ml_dtypes.float8_e5m2, 14)}[fmt]
    v = np.moveaxis(np.asarray(x, np.float32).astype(ml_dtypes.bfloat16).astype(np.float64), axis, -1)
    blocks = v.reshape(v.shape[:-1] + (-1, 32))
    amax = np.abs(blocks).max(-1, keepdims=True)
    byte = np.maximum(np.where(amax > 0, np.frexp(amax)[1] - 1 + 127, 0) - down, 1)
    scale = np.exp2(byte - 127.0)
    codes = (blocks / scale).astype(np.float32).astype(dtype).astype(np.float64)
    return np.moveaxis((codes * scale).reshape(v.shape), -1, axis)


WIDE = False


def mx_kscale(k):
    if not WIDE:
        return np.ones(k)
    levels = np.array([10, -10, 5, -5, 0])
    if k % 512:
        return np.exp2(np.random.permutation(np.resize(levels, k // 32))).repeat(32)
    a = np.empty((k // 512, 16))
    for p in range(k // 512):
        a[p, :8] = np.random.permutation(np.resize(levels, 8))
        for g in range(8):
            far = levels[np.abs(levels - a[p, g]) >= 10]
            a[p, g + 8] = far[np.random.randint(len(far))]
    return np.exp2(a.ravel()).repeat(32)


def f64(x):
    return np.asarray(x).astype(np.float64)


def striped(idx):
    return np.tile(idx.reshape(-1, 16).T, (8, 1)).astype(np.uint16)


def unstriped(offs):
    return offs[:16].T.reshape(-1).astype(np.int64)


def pack_weight(w):
    k, n = w.shape
    w = f64(np.asarray(w, np.float32).astype(ml_dtypes.bfloat16)).reshape(k // 32, 32, n)
    amax = np.abs(w).max(1)
    byte = np.clip(np.where(amax > 0, np.frexp(amax)[1] - 1 + 127 - 7, 1), 1, 254)
    scaled = (w * np.exp2(127.0 - byte)[:, None, :]).reshape(k, n).astype(np.float32)
    words = np.ascontiguousarray(scaled.reshape(k // 512, 128, 4, n).transpose(0, 1, 3, 2)).astype(ml_dtypes.float8_e4m3fn).view(np.uint8)
    return words, np.ascontiguousarray(byte.astype(np.uint8).reshape(k // 512, 16, n))


def unpack_weight(words, scales):
    g, p, n, _ = words.shape
    vals = np.ascontiguousarray(words).view(ml_dtypes.float8_e4m3fn).astype(np.float64) * np.repeat(np.exp2(scales.astype(np.float64) - 127.0), 8, axis=1)[..., None]
    return vals.transpose(0, 1, 3, 2).reshape(g * 512, n)


K, T, S, N, U = 512, 2048, 512, 128, 1024


def setup_inputs():
    n = np.random.standard_normal
    s = mx_kscale(K)[:, None]
    packed_xT = pack_weight(n((K, T)) * s)
    return {
        "x_words": packed_xT[0],
        "x_scales": packed_xT[1],
        "w1": (n((K, N)) / np.sqrt(K) / s).astype(np.float32),
        "vs": (np.random.uniform(0.1, 2.0, (N, U))).astype(np.float32),
        "ws": (n((N, U))).astype(np.float32),
        "offs": striped(np.random.permutation(T)[:S]),
        "slot": striped(np.random.permutation(U)[:S]),
    }


def reference(x_words, x_scales, w1, vs, ws, offs, slot):
    wsg = f64(ws)[:, unstriped(slot)]
    xq = unpack_weight(x_words, x_scales)[:, unstriped(offs)]
    y = mxq(f64(w1), 0, "e4m3").T @ xq
    vsg = f64(vs)[:, unstriped(slot)]
    vnew = 0.8 * vsg + 0.2 * ((y) ** 2)
    upd = y / (np.sqrt(vnew) + 0.1) + 0.1 * wsg
    wsq = (wsg) ** 2
    wnorm = np.sqrt(wsq.mean(axis=1, keepdims=True) + 0.01)
    u2 = (upd) ** 2
    unorm = np.sqrt(u2.mean(axis=1, keepdims=True) + 0.01)
    stp = (upd * wnorm) / unorm
    wput = wsg - (0.2 * stp)
    out = f64(ws).copy()
    out[:, unstriped(slot)] = wput
    return out

@@ -1,0 +1,135 @@
+import concourse.mybir as mybir
+
+K, T, S, N, U = 512, 2048, 512, 128, 1024
+FLOPS = 2 * K * S * N
+
+F32 = mybir.dt.float32
+BF16 = mybir.dt.bfloat16
+I32 = mybir.dt.int32
+U32 = mybir.dt.uint32
+U16 = mybir.dt.uint16
+U8 = mybir.dt.uint8
+FP8X4 = mybir.dt.float8_e4m3fn_x4
+ACT = mybir.ActivationFunctionType
+ALU = mybir.AluOpType
+
+P = 128
+PACK = 4
+HALF = S // 2
+LIST_COLS = S // 16
+NQ = 4
+
+
+def tile_picked_ylamb_put_p_kernel(tc, x_words, x_scales, w1, vs, ws, offs, slot, out):
+    nc = tc.nc
+    with (
+        tc.tile_pool(name="lists", bufs=1) as lists,
+        tc.tile_pool(name="sb", bufs=1) as sb,
+        tc.psum_pool(name="psum", bufs=1) as psum,
+    ):
+        offs_t = lists.tile([P, LIST_COLS], U16, name="offs_t")
+        slot_t = lists.tile([P, LIST_COLS], U16, name="slot_t")
+        words = sb.tile([P, T], U32, name="words", align_bytes=64)
+        scale_rows = sb.tile([P, T], U8, name="scale_rows", align_bytes=64)
+        w_raw = sb.tile([P, PACK, N], F32, name="w_raw")
+        vs_t = sb.tile([P, U], F32, name="vs_t")
+        ws_t = sb.tile([P, U], F32, name="ws_t")
+
+        nc.vector.memset(scale_rows[:, : T // 2].bitcast(I32), 0)
+        nc.gpsimd.memset(scale_rows[:, T // 2 :].bitcast(I32), 0)
+        nc.sync.dma_start(w_raw[:], w1.rearrange("(p j) n -> p j n", j=PACK))
+        nc.sync.dma_start(offs_t[:], offs)
+        for q in range(4):
+            queue = nc.sync if q < 2 else nc.scalar
+            queue.dma_start(scale_rows[32 * q : 32 * q + 4, :].bitcast(I32), x_scales[0, 4 * q : 4 * q + 4, :].bitcast(I32))
+        nc.sync.dma_start(words[:].bitcast(I32), x_words[0].rearrange("p n t -> p (n t)").bitcast(I32))
+        nc.sync.dma_start(slot_t[:], slot)
+        nc.sync.dma_start(ws_t[:], ws)
+        nc.sync.dma_start(vs_t[:], vs)
+
+        huge = sb.tile([P, 1], F32, name="huge")
+        guard = sb.tile([P, 1], F32, name="guard")
+        nc.vector.memset(huge[:], 2.0 ** 96)
+        nc.scalar.activation(guard[:], huge[:], ACT.Abs_reciprocal_sqrt)
+
+        picked_scales = sb.tile([P, S], U8, name="picked_scales", align_bytes=64)
+        nc.vector.tensor_copy(picked_scales[:], scale_rows[:].indirect(offs_t[:]))
+
+        w_bf = sb.tile([P, N, PACK], BF16, name="w_bf", align_bytes=64)
+        w_codes = sb.tile([P, N], U32, name="w_codes", align_bytes=64)
+        w_scales = sb.tile([P, N], U8, name="w_scales", align_bytes=64)
+        nc.scalar.copy(w_bf[:], w_raw[:].rearrange("p j n -> p n j"))
+        nc.vector.quantize_mx(out=w_codes[:].bitcast(FP8X4), scales=w_scales[:], in_=w_bf[:].rearrange("p n j -> p (n j)"))
+
+        def cols(i, n):
+            return slice(i * S // n, (i + 1) * S // n)
+
+        def list_cols(i, n):
+            return slice(i * LIST_COLS // n, (i + 1) * LIST_COLS // n)
+
+        def pieces(name, n, dtype=F32):
+            return [sb.tile([P, S // n], dtype, name=f"{name}{i}", align_bytes=64) for i in range(n)]
+
+        def column(name):
+            return sb.tile([P, 1], F32, name=name)
+
+        picked_words = pieces("picked_words", 2, U32)
+        y = [psum.tile([P, HALF], F32, name=f"y{h}") for h in range(2)]
+        ysq = sb.tile([P, S], F32, name="ysq")
+        v, a, t, rec, g = (pieces(n, NQ) for n in ("v", "a", "t", "rec", "g"))
+        wsg = sb.tile([P, S], F32, name="wsg")
+        upd = sb.tile([P, S], F32, name="upd")
+        wsq = sb.tile([P, S], F32, name="wsq")
+        usq = sb.tile([P, S], F32, name="usq")
+        step = sb.tile([P, S], F32, name="step")
+
+        for h in range(2):
+            nc.vector.tensor_copy(picked_words[h][:], words[:].indirect(offs_t[:, list_cols(h, 2)]))
+            nc.tensor.matmul_mx(out=y[h][:], lhsT=w_codes[:].bitcast(FP8X4), lhsT_scale=w_scales[:],
+                                rhs=picked_words[h][:].bitcast(FP8X4), rhs_scale=picked_scales[:, cols(h, 2)],
+                                start=True, stop=True)
+            nc.scalar.activation(ysq[:, cols(h, 2)], y[h][:], ACT.Square, scale=0.5)
+
+        wsum = [column(f"wsum{h}") for h in range(2)]
+        wpart, wmean, winv, wnorm = (column(n) for n in ("wpart", "wmean", "winv", "wnorm"))
+        for h in range(2):
+            nc.vector.tensor_copy(wsg[:, cols(h, 2)], ws_t[:].indirect(slot_t[:, list_cols(h, 2)]))
+            nc.scalar.activation(wsq[:, cols(h, 2)], wsg[:, cols(h, 2)], ACT.Square, accum_out=wsum[h][:])
+        nc.gpsimd.tensor_tensor(wpart[:], wsum[0][:], wsum[1][:], ALU.add)
+        nc.gpsimd.tensor_scalar(wmean[:], wpart[:], -1.0 / S, -0.01, ALU.mult, ALU.add)
+
+        for i in range(NQ):
+            nc.vector.tensor_tensor(v[i][:], vs_t[:].indirect(slot_t[:, list_cols(i, NQ)]), ysq[:, cols(i, NQ)], ALU.add)
+            nc.scalar.activation(a[i][:], v[i][:], ACT.Abs_reciprocal_sqrt, scale=0.8, bias=guard[:])
+        for i in range(NQ):
+            nc.vector.scalar_tensor_tensor(t[i][:], a[i][:], 5.0, v[i][:], ALU.add, ALU.mult)
+            nc.scalar.activation(rec[i][:], t[i][:], ACT.Abs_reciprocal_sqrt, scale=0.16, bias=0.01)
+        nc.scalar.activation(winv[:], wmean[:], ACT.Abs_reciprocal_sqrt)
+        nc.gpsimd.tensor_tensor(wnorm[:], wmean[:], winv[:], ALU.mult)
+
+        runs = [slice(0, S // 2), slice(S // 2, 3 * S // 4), slice(3 * S // 4, S)]
+        usum = [column(f"usum{r}") for r in range(3)]
+        ubias = [column(f"ubias{r}") for r in range(2)]
+        uinv = column("uinv")
+
+        def gradient(i):
+            y_i = y[i * 2 // NQ][:, (i * S // NQ) % HALF : (i * S // NQ) % HALF + S // NQ]
+            nc.vector.tensor_tensor(g[i][:], y_i, rec[i][:], ALU.mult)
+
+        def update(i):
+            nc.vector.scalar_tensor_tensor(upd[:, cols(i, NQ)], wsg[:, cols(i, NQ)], 0.1, g[i][:], ALU.mult, ALU.add)
+
+        gradient(0)
+        for i in range(1, NQ):
+            gradient(i)
+            update(i - 1)
+        update(NQ - 1)
+        for r in range(3):
+            nc.scalar.activation(usq[:, runs[r]], upd[:, runs[r]], ACT.Square, accum_out=usum[r][:])
+            if r > 0:
+                nc.scalar.activation(ubias[r - 1][:], usum[r - 1][:], ACT.Identity, scale=25.0 / S,
+                                     bias=0.25 if r == 1 else ubias[r - 2][:])
+        nc.scalar.activation(uinv[:], usum[2][:], ACT.Abs_reciprocal_sqrt, scale=25.0 / S, bias=ubias[1][:])
+        nc.vector.tensor_scalar(step[:], upd[:], uinv[:], wnorm[:], ALU.mult, ALU.mult)
+        nc.vector.tensor_tensor(ws_t[:].indirect(slot_t[:]), step[:], wsg[:], ALU.add)
+        nc.sync.dma_start(out, ws_t[:])

@@ -18,6 +18,7 @@ PACK = 4
 HALF = S // 2
 LIST_COLS = S // 16
 NQ = 4
+EARLY = 768
 
 
 def tile_picked_ylamb_put_p_kernel(tc, x_words, x_scales, w1, vs, ws, offs, slot, out):
@@ -39,10 +40,11 @@ def tile_picked_ylamb_put_p_kernel(tc, x_words, x_scales, w1, vs, ws, offs, slot
         nc.gpsimd.memset(scale_rows[:, T // 2 :].bitcast(I32), 0)
         nc.sync.dma_start(w_raw[:], w1.rearrange("(p j) n -> p j n", j=PACK))
         nc.sync.dma_start(offs_t[:], offs)
+        words_hbm = x_words[0].rearrange("p n t -> p (n t)").bitcast(I32)
+        nc.sync.dma_start(words[:, :EARLY].bitcast(I32), words_hbm[:, :EARLY])
         for q in range(4):
-            queue = nc.sync if q < 2 else nc.scalar
-            queue.dma_start(scale_rows[32 * q : 32 * q + 4, :].bitcast(I32), x_scales[0, 4 * q : 4 * q + 4, :].bitcast(I32))
-        nc.sync.dma_start(words[:].bitcast(I32), x_words[0].rearrange("p n t -> p (n t)").bitcast(I32))
+            nc.sync.dma_start(scale_rows[32 * q : 32 * q + 4, :].bitcast(I32), x_scales[0, 4 * q : 4 * q + 4, :].bitcast(I32))
+        nc.sync.dma_start(words[:, EARLY:].bitcast(I32), words_hbm[:, EARLY:])
         nc.sync.dma_start(slot_t[:], slot)
         nc.sync.dma_start(ws_t[:], ws)
         nc.sync.dma_start(vs_t[:], vs)
@@ -76,7 +78,8 @@ def tile_picked_ylamb_put_p_kernel(tc, x_words, x_scales, w1, vs, ws, offs, slot
         picked_words = pieces("picked_words", 2, U32)
         y = [psum.tile([P, HALF], F32, name=f"y{h}") for h in range(2)]
         ysq = sb.tile([P, S], F32, name="ysq")
-        v, a, t, rec, g = (pieces(n, NQ) for n in ("v", "a", "t", "rec", "g"))
+        v, a, t, rec = (pieces(n, NQ) for n in ("v", "a", "t", "rec"))
+        g = sb.tile([P, S], F32, name="g")
         wsg = sb.tile([P, S], F32, name="wsg")
         upd = sb.tile([P, S], F32, name="upd")
         wsq = sb.tile([P, S], F32, name="wsq")
@@ -90,13 +93,12 @@ def tile_picked_ylamb_put_p_kernel(tc, x_words, x_scales, w1, vs, ws, offs, slot
                                 start=True, stop=True)
             nc.scalar.activation(ysq[:, cols(h, 2)], y[h][:], ACT.Square, scale=0.5)
 
-        wsum = [column(f"wsum{h}") for h in range(2)]
-        wpart, wmean, winv, wnorm = (column(n) for n in ("wpart", "wmean", "winv", "wnorm"))
-        for h in range(2):
-            nc.vector.tensor_copy(wsg[:, cols(h, 2)], ws_t[:].indirect(slot_t[:, list_cols(h, 2)]))
-            nc.scalar.activation(wsq[:, cols(h, 2)], wsg[:, cols(h, 2)], ACT.Square, accum_out=wsum[h][:])
-        nc.gpsimd.tensor_tensor(wpart[:], wsum[0][:], wsum[1][:], ALU.add)
-        nc.gpsimd.tensor_scalar(wmean[:], wpart[:], -1.0 / S, -0.01, ALU.mult, ALU.add)
+        wsum, wmean, winv, wnorm = (column(n) for n in ("wsum", "wmean", "winv", "wnorm"))
+        nc.vector.tensor_copy(wsg[:], ws_t[:].indirect(slot_t[:]))
+        nc.scalar.activation(wsq[:], wsg[:], ACT.Square, accum_out=wsum[:])
+        nc.scalar.activation(wmean[:], wsum[:], ACT.Copy, scale=-1.0 / S, bias=-0.01)
+        nc.scalar.activation(winv[:], wmean[:], ACT.Abs_reciprocal_sqrt)
+        nc.scalar.activation(wnorm[:], wmean[:], ACT.Copy, scale=winv[:])
 
         for i in range(NQ):
             nc.vector.tensor_tensor(v[i][:], vs_t[:].indirect(slot_t[:, list_cols(i, NQ)]), ysq[:, cols(i, NQ)], ALU.add)
@@ -104,8 +106,6 @@ def tile_picked_ylamb_put_p_kernel(tc, x_words, x_scales, w1, vs, ws, offs, slot
         for i in range(NQ):
             nc.vector.scalar_tensor_tensor(t[i][:], a[i][:], 5.0, v[i][:], ALU.add, ALU.mult)
             nc.scalar.activation(rec[i][:], t[i][:], ACT.Abs_reciprocal_sqrt, scale=0.16, bias=0.01)
-        nc.scalar.activation(winv[:], wmean[:], ACT.Abs_reciprocal_sqrt)
-        nc.gpsimd.tensor_tensor(wnorm[:], wmean[:], winv[:], ALU.mult)
 
         runs = [slice(0, S // 2), slice(S // 2, 3 * S // 4), slice(3 * S // 4, S)]
         usum = [column(f"usum{r}") for r in range(3)]
@@ -114,21 +114,21 @@ def tile_picked_ylamb_put_p_kernel(tc, x_words, x_scales, w1, vs, ws, offs, slot
 
         def gradient(i):
             y_i = y[i * 2 // NQ][:, (i * S // NQ) % HALF : (i * S // NQ) % HALF + S // NQ]
-            nc.vector.tensor_tensor(g[i][:], y_i, rec[i][:], ALU.mult)
+            nc.vector.tensor_tensor(g[:, cols(i, NQ)], y_i, rec[i][:], ALU.mult)
 
-        def update(i):
-            nc.vector.scalar_tensor_tensor(upd[:, cols(i, NQ)], wsg[:, cols(i, NQ)], 0.1, g[i][:], ALU.mult, ALU.add)
+        def update(r):
+            nc.vector.scalar_tensor_tensor(upd[:, runs[r]], wsg[:, runs[r]], 0.1, g[:, runs[r]], ALU.mult, ALU.add)
+            nc.scalar.activation(usq[:, runs[r]], upd[:, runs[r]], ACT.Square, accum_out=usum[r][:])
 
         gradient(0)
-        for i in range(1, NQ):
-            gradient(i)
-            update(i - 1)
-        update(NQ - 1)
-        for r in range(3):
-            nc.scalar.activation(usq[:, runs[r]], upd[:, runs[r]], ACT.Square, accum_out=usum[r][:])
-            if r > 0:
-                nc.scalar.activation(ubias[r - 1][:], usum[r - 1][:], ACT.Identity, scale=25.0 / S,
-                                     bias=0.25 if r == 1 else ubias[r - 2][:])
+        gradient(1)
+        gradient(2)
+        update(0)
+        gradient(3)
+        update(1)
+        update(2)
+        nc.vector.tensor_scalar(ubias[0][:], usum[0][:], 25.0 / S, 0.25, ALU.mult, ALU.add)
+        nc.vector.scalar_tensor_tensor(ubias[1][:], usum[1][:], 25.0 / S, ubias[0][:], ALU.mult, ALU.add)
         nc.scalar.activation(uinv[:], usum[2][:], ACT.Abs_reciprocal_sqrt, scale=25.0 / S, bias=ubias[1][:])
         nc.vector.tensor_scalar(step[:], upd[:], uinv[:], wnorm[:], ALU.mult, ALU.mult)
         nc.vector.tensor_tensor(ws_t[:].indirect(slot_t[:]), step[:], wsg[:], ALU.add)

@@ -18,7 +18,7 @@ PACK = 4
 HALF = S // 2
 LIST_COLS = S // 16
 NQ = 4
-EARLY = 768
+EARLY = 512
 
 
 def tile_picked_ylamb_put_p_kernel(tc, x_words, x_scales, w1, vs, ws, offs, slot, out):
@@ -36,14 +36,13 @@ def tile_picked_ylamb_put_p_kernel(tc, x_words, x_scales, w1, vs, ws, offs, slot
         vs_t = sb.tile([P, U], F32, name="vs_t")
         ws_t = sb.tile([P, U], F32, name="ws_t")
 
-        nc.vector.memset(scale_rows[:, : T // 2].bitcast(I32), 0)
-        nc.gpsimd.memset(scale_rows[:, T // 2 :].bitcast(I32), 0)
+        nc.vector.memset(scale_rows[:].bitcast(I32), 0)
         nc.sync.dma_start(w_raw[:], w1.rearrange("(p j) n -> p j n", j=PACK))
         nc.sync.dma_start(offs_t[:], offs)
         words_hbm = x_words[0].rearrange("p n t -> p (n t)").bitcast(I32)
         nc.sync.dma_start(words[:, :EARLY].bitcast(I32), words_hbm[:, :EARLY])
-        for q in range(4):
-            nc.sync.dma_start(scale_rows[32 * q : 32 * q + 4, :].bitcast(I32), x_scales[0, 4 * q : 4 * q + 4, :].bitcast(I32))
+        for r in range(4):
+            nc.sync.dma_start(scale_rows[r:P:32, :].bitcast(I32), x_scales[0, r:16:4, :].bitcast(I32))
         nc.sync.dma_start(words[:, EARLY:].bitcast(I32), words_hbm[:, EARLY:])
         nc.sync.dma_start(slot_t[:], slot)
         nc.sync.dma_start(ws_t[:], ws)

@@ -15,10 +15,13 @@ ALU = mybir.AluOpType
 
 P = 128
 PACK = 4
-HALF = S // 2
+QUADRANT = 32
+SCALE_ROWS = 4
 LIST_COLS = S // 16
-NQ = 4
-EARLY = 512
+HALVES = 2
+QUARTERS = 4
+HALF, QUARTER = S // HALVES, S // QUARTERS
+EARLY_WORDS = 512
 
 
 def tile_picked_ylamb_put_p_kernel(tc, x_words, x_scales, w1, vs, ws, offs, slot, out):
@@ -28,6 +31,19 @@ def tile_picked_ylamb_put_p_kernel(tc, x_words, x_scales, w1, vs, ws, offs, slot
         tc.tile_pool(name="sb", bufs=1) as sb,
         tc.psum_pool(name="psum", bufs=1) as psum,
     ):
+
+        def entries(i, parts):
+            return slice(i * S // parts, (i + 1) * S // parts)
+
+        def list_cols(i, parts):
+            return slice(i * LIST_COLS // parts, (i + 1) * LIST_COLS // parts)
+
+        def quarter_tiles(name):
+            return [sb.tile([P, QUARTER], F32, name=f"{name}{i}", align_bytes=64) for i in range(QUARTERS)]
+
+        def column(name):
+            return sb.tile([P, 1], F32, name=name)
+
         offs_t = lists.tile([P, LIST_COLS], U16, name="offs_t")
         slot_t = lists.tile([P, LIST_COLS], U16, name="slot_t")
         words = sb.tile([P, T], U32, name="words", align_bytes=64)
@@ -40,18 +56,17 @@ def tile_picked_ylamb_put_p_kernel(tc, x_words, x_scales, w1, vs, ws, offs, slot
         nc.sync.dma_start(w_raw[:], w1.rearrange("(p j) n -> p j n", j=PACK))
         nc.sync.dma_start(offs_t[:], offs)
         words_hbm = x_words[0].rearrange("p n t -> p (n t)").bitcast(I32)
-        nc.sync.dma_start(words[:, :EARLY].bitcast(I32), words_hbm[:, :EARLY])
-        for r in range(4):
-            nc.sync.dma_start(scale_rows[r:P:32, :].bitcast(I32), x_scales[0, r:16:4, :].bitcast(I32))
-        nc.sync.dma_start(words[:, EARLY:].bitcast(I32), words_hbm[:, EARLY:])
+        nc.sync.dma_start(words[:, :EARLY_WORDS].bitcast(I32), words_hbm[:, :EARLY_WORDS])
+        for r in range(SCALE_ROWS):
+            nc.sync.dma_start(scale_rows[r:P:QUADRANT, :].bitcast(I32), x_scales[0, r : K // 32 : SCALE_ROWS, :].bitcast(I32))
+        nc.sync.dma_start(words[:, EARLY_WORDS:].bitcast(I32), words_hbm[:, EARLY_WORDS:])
         nc.sync.dma_start(slot_t[:], slot)
         nc.sync.dma_start(ws_t[:], ws)
         nc.sync.dma_start(vs_t[:], vs)
 
-        huge = sb.tile([P, 1], F32, name="huge")
-        guard = sb.tile([P, 1], F32, name="guard")
-        nc.vector.memset(huge[:], 2.0 ** 96)
-        nc.scalar.activation(guard[:], huge[:], ACT.Abs_reciprocal_sqrt)
+        huge, tiny = column("huge"), column("tiny")
+        nc.vector.memset(huge[:], 2.0**96)
+        nc.scalar.activation(tiny[:], huge[:], ACT.Abs_reciprocal_sqrt)
 
         picked_scales = sb.tile([P, S], U8, name="picked_scales", align_bytes=64)
         nc.vector.tensor_copy(picked_scales[:], scale_rows[:].indirect(offs_t[:]))
@@ -62,73 +77,61 @@ def tile_picked_ylamb_put_p_kernel(tc, x_words, x_scales, w1, vs, ws, offs, slot
         nc.scalar.copy(w_bf[:], w_raw[:].rearrange("p j n -> p n j"))
         nc.vector.quantize_mx(out=w_codes[:].bitcast(FP8X4), scales=w_scales[:], in_=w_bf[:].rearrange("p n j -> p (n j)"))
 
-        def cols(i, n):
-            return slice(i * S // n, (i + 1) * S // n)
-
-        def list_cols(i, n):
-            return slice(i * LIST_COLS // n, (i + 1) * LIST_COLS // n)
-
-        def pieces(name, n, dtype=F32):
-            return [sb.tile([P, S // n], dtype, name=f"{name}{i}", align_bytes=64) for i in range(n)]
-
-        def column(name):
-            return sb.tile([P, 1], F32, name=name)
-
-        picked_words = pieces("picked_words", 2, U32)
-        y = [psum.tile([P, HALF], F32, name=f"y{h}") for h in range(2)]
+        picked_words = [sb.tile([P, HALF], U32, name=f"picked_words{h}", align_bytes=64) for h in range(HALVES)]
+        y = [psum.tile([P, HALF], F32, name=f"y{h}") for h in range(HALVES)]
         ysq = sb.tile([P, S], F32, name="ysq")
-        v, a, t, rec = (pieces(n, NQ) for n in ("v", "a", "t", "rec"))
-        g = sb.tile([P, S], F32, name="g")
+        v, root_inv, denom_sq, denom_inv = (quarter_tiles(n) for n in ("v", "root_inv", "denom_sq", "denom_inv"))
+        grad = sb.tile([P, S], F32, name="grad")
         wsg = sb.tile([P, S], F32, name="wsg")
         upd = sb.tile([P, S], F32, name="upd")
         wsq = sb.tile([P, S], F32, name="wsq")
         usq = sb.tile([P, S], F32, name="usq")
         step = sb.tile([P, S], F32, name="step")
 
-        for h in range(2):
-            nc.vector.tensor_copy(picked_words[h][:], words[:].indirect(offs_t[:, list_cols(h, 2)]))
-            nc.tensor.matmul_mx(out=y[h][:], lhsT=w_codes[:].bitcast(FP8X4), lhsT_scale=w_scales[:],
-                                rhs=picked_words[h][:].bitcast(FP8X4), rhs_scale=picked_scales[:, cols(h, 2)],
-                                start=True, stop=True)
-            nc.scalar.activation(ysq[:, cols(h, 2)], y[h][:], ACT.Square, scale=0.5)
+        for h in range(HALVES):
+            nc.vector.tensor_copy(picked_words[h][:], words[:].indirect(offs_t[:, list_cols(h, HALVES)]))
+            nc.tensor.matmul_mx(
+                out=y[h][:],
+                lhsT=w_codes[:].bitcast(FP8X4),
+                lhsT_scale=w_scales[:],
+                rhs=picked_words[h][:].bitcast(FP8X4),
+                rhs_scale=picked_scales[:, entries(h, HALVES)],
+                start=True,
+                stop=True,
+            )
+            nc.scalar.activation(ysq[:, entries(h, HALVES)], y[h][:], ACT.Square, scale=0.5)
 
-        wsum, wmean, winv, wnorm = (column(n) for n in ("wsum", "wmean", "winv", "wnorm"))
+        wsum, w_factor = column("wsum"), column("w_factor")
         nc.vector.tensor_copy(wsg[:], ws_t[:].indirect(slot_t[:]))
         nc.scalar.activation(wsq[:], wsg[:], ACT.Square, accum_out=wsum[:])
-        nc.scalar.activation(wmean[:], wsum[:], ACT.Copy, scale=-1.0 / S, bias=-0.01)
-        nc.scalar.activation(winv[:], wmean[:], ACT.Abs_reciprocal_sqrt)
-        nc.scalar.activation(wnorm[:], wmean[:], ACT.Copy, scale=winv[:])
 
-        for i in range(NQ):
-            nc.vector.tensor_tensor(v[i][:], vs_t[:].indirect(slot_t[:, list_cols(i, NQ)]), ysq[:, cols(i, NQ)], ALU.add)
-            nc.scalar.activation(a[i][:], v[i][:], ACT.Abs_reciprocal_sqrt, scale=0.8, bias=guard[:])
-        for i in range(NQ):
-            nc.vector.scalar_tensor_tensor(t[i][:], a[i][:], 5.0, v[i][:], ALU.add, ALU.mult)
-            nc.scalar.activation(rec[i][:], t[i][:], ACT.Abs_reciprocal_sqrt, scale=0.16, bias=0.01)
+        for i in range(QUARTERS):
+            nc.vector.tensor_tensor(v[i][:], vs_t[:].indirect(slot_t[:, list_cols(i, QUARTERS)]), ysq[:, entries(i, QUARTERS)], ALU.add)
+            nc.scalar.activation(root_inv[i][:], v[i][:], ACT.Abs_reciprocal_sqrt, scale=0.8, bias=tiny[:])
+        for i in range(QUARTERS):
+            nc.vector.scalar_tensor_tensor(denom_sq[i][:], root_inv[i][:], 5.0, v[i][:], ALU.add, ALU.mult)
+            nc.scalar.activation(denom_inv[i][:], denom_sq[i][:], ACT.Abs_reciprocal_sqrt, scale=0.16, bias=0.01)
 
-        runs = [slice(0, S // 2), slice(S // 2, 3 * S // 4), slice(3 * S // 4, S)]
-        usum = [column(f"usum{r}") for r in range(3)]
-        ubias = [column(f"ubias{r}") for r in range(2)]
-        uinv = column("uinv")
+        wmean_neg, wmean_inv_root = denom_sq[-1][:, 0:1], denom_sq[-1][:, 1:2]
+        nc.scalar.activation(wmean_inv_root, wsum[:], ACT.Abs_reciprocal_sqrt, scale=1.0 / S, bias=0.01)
+        nc.scalar.activation(wmean_neg, wsum[:], ACT.Copy, scale=-1.0 / S, bias=-0.01)
+        nc.scalar.activation(w_factor[:], wmean_neg, ACT.Copy, scale=wmean_inv_root)
 
-        def gradient(i):
-            y_i = y[i * 2 // NQ][:, (i * S // NQ) % HALF : (i * S // NQ) % HALF + S // NQ]
-            nc.vector.tensor_tensor(g[:, cols(i, NQ)], y_i, rec[i][:], ALU.mult)
+        usum = [column(f"usum{h}") for h in range(HALVES)]
+        first_half_term, u_factor = column("first_half_term"), column("u_factor")
+        for i in range(QUARTERS):
+            h, start = divmod(i * QUARTER, HALF)
+            nc.vector.tensor_tensor(grad[:, entries(i, QUARTERS)], y[h][:, start : start + QUARTER], denom_inv[i][:], ALU.mult)
+        for h in range(HALVES):
+            c = entries(h, HALVES)
+            nc.vector.scalar_tensor_tensor(upd[:, c], wsg[:, c], 0.1, grad[:, c], ALU.mult, ALU.add)
+        for h in range(HALVES):
+            c = entries(h, HALVES)
+            nc.scalar.activation(usq[:, c], upd[:, c], ACT.Square, accum_out=usum[h][:])
 
-        def update(r):
-            nc.vector.scalar_tensor_tensor(upd[:, runs[r]], wsg[:, runs[r]], 0.1, g[:, runs[r]], ALU.mult, ALU.add)
-            nc.scalar.activation(usq[:, runs[r]], upd[:, runs[r]], ACT.Square, accum_out=usum[r][:])
+        nc.vector.tensor_scalar(first_half_term[:], usum[0][:], 25.0 / S, 0.25, ALU.mult, ALU.add)
+        nc.scalar.activation(u_factor[:], usum[1][:], ACT.Abs_reciprocal_sqrt, scale=25.0 / S, bias=first_half_term[:])
 
-        gradient(0)
-        gradient(1)
-        gradient(2)
-        update(0)
-        gradient(3)
-        update(1)
-        update(2)
-        nc.vector.tensor_scalar(ubias[0][:], usum[0][:], 25.0 / S, 0.25, ALU.mult, ALU.add)
-        nc.vector.scalar_tensor_tensor(ubias[1][:], usum[1][:], 25.0 / S, ubias[0][:], ALU.mult, ALU.add)
-        nc.scalar.activation(uinv[:], usum[2][:], ACT.Abs_reciprocal_sqrt, scale=25.0 / S, bias=ubias[1][:])
-        nc.vector.tensor_scalar(step[:], upd[:], uinv[:], wnorm[:], ALU.mult, ALU.mult)
+        nc.vector.tensor_scalar(step[:], upd[:], u_factor[:], w_factor[:], ALU.mult, ALU.mult)
         nc.vector.tensor_tensor(ws_t[:].indirect(slot_t[:]), step[:], wsg[:], ALU.add)
         nc.sync.dma_start(out, ws_t[:])

import concourse.mybir as mybir

K, T, S, N, U = 512, 2048, 512, 128, 1024
FLOPS = 2 * K * S * N

F32 = mybir.dt.float32
BF16 = mybir.dt.bfloat16
I32 = mybir.dt.int32
U32 = mybir.dt.uint32
U16 = mybir.dt.uint16
U8 = mybir.dt.uint8
FP8X4 = mybir.dt.float8_e4m3fn_x4
ACT = mybir.ActivationFunctionType
ALU = mybir.AluOpType

P = 128
PACK = 4
QUADRANT = 32
SCALE_ROWS = 4
LIST_COLS = S // 16
HALVES = 2
QUARTERS = 4
HALF, QUARTER = S // HALVES, S // QUARTERS
EARLY_WORDS = 512


def tile_picked_ylamb_put_p_kernel(tc, x_words, x_scales, w1, vs, ws, offs, slot, out):
    nc = tc.nc
    with (
        tc.tile_pool(name="lists", bufs=1) as lists,
        tc.tile_pool(name="sb", bufs=1) as sb,
        tc.psum_pool(name="psum", bufs=1) as psum,
    ):

        def entries(i, parts):
            return slice(i * S // parts, (i + 1) * S // parts)

        def list_cols(i, parts):
            return slice(i * LIST_COLS // parts, (i + 1) * LIST_COLS // parts)

        def quarter_tiles(name):
            return [sb.tile([P, QUARTER], F32, name=f"{name}{i}", align_bytes=64) for i in range(QUARTERS)]

        def column(name):
            return sb.tile([P, 1], F32, name=name)

        offs_t = lists.tile([P, LIST_COLS], U16, name="offs_t")
        slot_t = lists.tile([P, LIST_COLS], U16, name="slot_t")
        words = sb.tile([P, T], U32, name="words", align_bytes=64)
        scale_rows = sb.tile([P, T], U8, name="scale_rows", align_bytes=64)
        w_raw = sb.tile([P, PACK, N], F32, name="w_raw")
        vs_t = sb.tile([P, U], F32, name="vs_t")
        ws_t = sb.tile([P, U], F32, name="ws_t")

        nc.vector.memset(scale_rows[:].bitcast(I32), 0)
        nc.sync.dma_start(w_raw[:], w1.rearrange("(p j) n -> p j n", j=PACK))
        nc.sync.dma_start(offs_t[:], offs)
        words_hbm = x_words[0].rearrange("p n t -> p (n t)").bitcast(I32)
        nc.sync.dma_start(words[:, :EARLY_WORDS].bitcast(I32), words_hbm[:, :EARLY_WORDS])
        for r in range(SCALE_ROWS):
            nc.sync.dma_start(scale_rows[r:P:QUADRANT, :].bitcast(I32), x_scales[0, r : K // 32 : SCALE_ROWS, :].bitcast(I32))
        nc.sync.dma_start(words[:, EARLY_WORDS:].bitcast(I32), words_hbm[:, EARLY_WORDS:])
        nc.sync.dma_start(slot_t[:], slot)
        nc.sync.dma_start(ws_t[:], ws)
        nc.sync.dma_start(vs_t[:], vs)

        huge, tiny = column("huge"), column("tiny")
        nc.vector.memset(huge[:], 2.0**96)
        nc.scalar.activation(tiny[:], huge[:], ACT.Abs_reciprocal_sqrt)

        picked_scales = sb.tile([P, S], U8, name="picked_scales", align_bytes=64)
        nc.vector.tensor_copy(picked_scales[:], scale_rows[:].indirect(offs_t[:]))

        w_bf = sb.tile([P, N, PACK], BF16, name="w_bf", align_bytes=64)
        w_codes = sb.tile([P, N], U32, name="w_codes", align_bytes=64)
        w_scales = sb.tile([P, N], U8, name="w_scales", align_bytes=64)
        nc.scalar.copy(w_bf[:], w_raw[:].rearrange("p j n -> p n j"))
        nc.vector.quantize_mx(out=w_codes[:].bitcast(FP8X4), scales=w_scales[:], in_=w_bf[:].rearrange("p n j -> p (n j)"))

        picked_words = [sb.tile([P, HALF], U32, name=f"picked_words{h}", align_bytes=64) for h in range(HALVES)]
        y = [psum.tile([P, HALF], F32, name=f"y{h}") for h in range(HALVES)]
        ysq = sb.tile([P, S], F32, name="ysq")
        v, root_inv, denom_sq, denom_inv = (quarter_tiles(n) for n in ("v", "root_inv", "denom_sq", "denom_inv"))
        grad = sb.tile([P, S], F32, name="grad")
        wsg = sb.tile([P, S], F32, name="wsg")
        upd = sb.tile([P, S], F32, name="upd")
        wsq = sb.tile([P, S], F32, name="wsq")
        usq = sb.tile([P, S], F32, name="usq")
        step = sb.tile([P, S], F32, name="step")

        for h in range(HALVES):
            nc.vector.tensor_copy(picked_words[h][:], words[:].indirect(offs_t[:, list_cols(h, HALVES)]))
            nc.tensor.matmul_mx(
                out=y[h][:],
                lhsT=w_codes[:].bitcast(FP8X4),
                lhsT_scale=w_scales[:],
                rhs=picked_words[h][:].bitcast(FP8X4),
                rhs_scale=picked_scales[:, entries(h, HALVES)],
                start=True,
                stop=True,
            )
            nc.scalar.activation(ysq[:, entries(h, HALVES)], y[h][:], ACT.Square, scale=0.5)

        wsum, w_factor = column("wsum"), column("w_factor")
        nc.vector.tensor_copy(wsg[:], ws_t[:].indirect(slot_t[:]))
        nc.scalar.activation(wsq[:], wsg[:], ACT.Square, accum_out=wsum[:])

        for i in range(QUARTERS):
            nc.vector.tensor_tensor(v[i][:], vs_t[:].indirect(slot_t[:, list_cols(i, QUARTERS)]), ysq[:, entries(i, QUARTERS)], ALU.add)
            nc.scalar.activation(root_inv[i][:], v[i][:], ACT.Abs_reciprocal_sqrt, scale=0.8, bias=tiny[:])
        for i in range(QUARTERS):
            nc.vector.scalar_tensor_tensor(denom_sq[i][:], root_inv[i][:], 5.0, v[i][:], ALU.add, ALU.mult)
            nc.scalar.activation(denom_inv[i][:], denom_sq[i][:], ACT.Abs_reciprocal_sqrt, scale=0.16, bias=0.01)

        wmean_neg, wmean_inv_root = denom_sq[-1][:, 0:1], denom_sq[-1][:, 1:2]
        nc.scalar.activation(wmean_inv_root, wsum[:], ACT.Abs_reciprocal_sqrt, scale=1.0 / S, bias=0.01)
        nc.scalar.activation(wmean_neg, wsum[:], ACT.Copy, scale=-1.0 / S, bias=-0.01)
        nc.scalar.activation(w_factor[:], wmean_neg, ACT.Copy, scale=wmean_inv_root)

        usum = [column(f"usum{h}") for h in range(HALVES)]
        first_half_term, u_factor = column("first_half_term"), column("u_factor")
        for i in range(QUARTERS):
            h, start = divmod(i * QUARTER, HALF)
            nc.vector.tensor_tensor(grad[:, entries(i, QUARTERS)], y[h][:, start : start + QUARTER], denom_inv[i][:], ALU.mult)
        for h in range(HALVES):
            c = entries(h, HALVES)
            nc.vector.scalar_tensor_tensor(upd[:, c], wsg[:, c], 0.1, grad[:, c], ALU.mult, ALU.add)
        for h in range(HALVES):
            c = entries(h, HALVES)
            nc.scalar.activation(usq[:, c], upd[:, c], ACT.Square, accum_out=usum[h][:])

        nc.vector.tensor_scalar(first_half_term[:], usum[0][:], 25.0 / S, 0.25, ALU.mult, ALU.add)
        nc.scalar.activation(u_factor[:], usum[1][:], ACT.Abs_reciprocal_sqrt, scale=25.0 / S, bias=first_half_term[:])

        nc.vector.tensor_scalar(step[:], upd[:], u_factor[:], w_factor[:], ALU.mult, ALU.mult)
        nc.vector.tensor_tensor(ws_t[:].indirect(slot_t[:]), step[:], wsg[:], ALU.add)
        nc.sync.dma_start(out, ws_t[:])
